import numpy as np
import ml_dtypes


def mxq(x, axis, fmt="e4m3"):
    dtype, down = {"e4m3": (ml_dtypes.float8_e4m3fn, 7), "e5m2": (ml_dtypes.float8_e5m2, 14)}[fmt]
    v = np.moveaxis(np.asarray(x, np.float32).astype(ml_dtypes.bfloat16).astype(np.float64), axis, -1)
    blocks = v.reshape(v.shape[:-1] + (-1, 32))
    amax = np.abs(blocks).max(-1, keepdims=True)
    byte = np.maximum(np.where(amax > 0, np.frexp(amax)[1] - 1 + 127, 0) - down, 1)
    scale = np.exp2(byte - 127.0)
    codes = (blocks / scale).astype(np.float32).astype(dtype).astype(np.float64)
    return np.moveaxis((codes * scale).reshape(v.shape), -1, axis)


WIDE = False


def mx_kscale(k):
    if not WIDE:
        return np.ones(k)
    levels = np.array([10, -10, 5, -5, 0])
    if k % 512:
        return np.exp2(np.random.permutation(np.resize(levels, k // 32))).repeat(32)
    a = np.empty((k // 512, 16))
    for p in range(k // 512):
        a[p, :8] = np.random.permutation(np.resize(levels, 8))
        for g in range(8):
            far = levels[np.abs(levels - a[p, g]) >= 10]
            a[p, g + 8] = far[np.random.randint(len(far))]
    return np.exp2(a.ravel()).repeat(32)


def f64(x):
    return np.asarray(x).astype(np.float64)


def striped(idx):
    return np.tile(np.asarray(idx).reshape(-1, 16).T, (8, 1)).astype(np.uint16)


def unstriped(offs):
    return offs[:16].T.reshape(-1).astype(np.int64)


def striped8(idx):
    return np.asarray(idx).reshape(8, -1, 16).transpose(0, 2, 1).reshape(128, -1).astype(np.uint16)


def unstriped8(offs):
    return offs.reshape(8, 16, -1).transpose(0, 2, 1).reshape(8, -1).astype(np.int64)


def pick8(x, idx, run):
    r = np.arange(len(x))
    return x[r[:, None], idx[r % (8 * run) // run]]


E2M1 = np.array([0.0, 0.5, 1.0, 1.5, 2.0, 3.0, 4.0, 6.0, -0.0, -0.5, -1.0, -1.5, -2.0, -3.0, -4.0, -6.0])


def pack_weight(w, fmt):
    k, n = w.shape
    w = f64(np.asarray(w, np.float32).astype(ml_dtypes.bfloat16)).reshape(k // 32, 32, n)
    amax = np.abs(w).max(1)
    if fmt == "e4m3":
        byte = np.frexp(amax)[1] - 1 + 127 - 7
    else:
        mant, ex = np.frexp(amax / 6.0)
        byte = np.where(mant > 0.5, ex, ex - 1) + 127
    byte = np.clip(np.where(amax > 0, byte, 1), 1, 254)
    scaled = (w * np.exp2(127.0 - byte)[:, None, :]).reshape(k, n).astype(np.float32)
    by_word = np.ascontiguousarray(scaled.reshape(k // 512, 128, 4, n).transpose(0, 1, 3, 2))
    if fmt == "e4m3":
        words = by_word.astype(ml_dtypes.float8_e4m3fn).view(np.uint8)
    else:
        c = by_word.astype(ml_dtypes.float4_e2m1fn).view(np.uint8) & 0xF
        words = (c[..., 0::2] | (c[..., 1::2] << 4)).reshape(k // 512, 128, 2 * n)
    return np.ascontiguousarray(words), np.ascontiguousarray(byte.astype(np.uint8).reshape(k // 512, 16, n))


def unpack_weight(words, scales, fmt):
    g, _, n = scales.shape
    words = np.ascontiguousarray(words).reshape(g, 128, n, -1)
    if fmt == "e4m3":
        vals = words.view(ml_dtypes.float8_e4m3fn).astype(np.float64)
    else:
        nib = np.empty((g, 128, n, 4), np.uint8)
        nib[..., 0::2] = words & 0xF
        nib[..., 1::2] = words >> 4
        vals = E2M1[nib]
    vals = vals * np.repeat(np.exp2(scales.astype(np.float64) - 127.0), 8, axis=1)[..., None]
    return vals.transpose(0, 1, 3, 2).reshape(g * 512, n)


K, J, R, T, C, D, O, N, S = 512, 256, 512, 512, 512, 1024, 256, 256, 1024


def setup_inputs():
    n = np.random.standard_normal
    idx = np.random.permutation(T)[:J]
    idx2 = np.stack([np.random.permutation(C)[:J] for _ in range(8)])
    idx3 = np.stack([np.random.permutation(C)[:J] for _ in range(8)])
    idx4 = np.stack([np.random.permutation(D)[:C] for _ in range(8)])
    idx5 = np.stack([np.random.permutation(D)[:O] for _ in range(8)])
    idx6 = np.random.permutation(S)[:N]
    fk = mx_kscale(K)
    fr = mx_kscale(R)
    xtp = pack_weight(n((K, T)) * fk[:, None], "e4m3")
    wp = pack_weight(n((K, R)) * 1 / np.sqrt(K) / fk[:, None] * fr, "e2m1")
    w2p = pack_weight(n((K, R)) * 1 / np.sqrt(K) / fk[:, None] * fr, "e4m3")
    vsp = pack_weight(n((R, S)) * 1 / np.sqrt(R) / fr[:, None], "e4m3")
    return {
        "xt_words": xtp[0],
        "xt_scales": xtp[1],
        "w_words": wp[0],
        "w_scales": wp[1],
        "w2_words": w2p[0],
        "w2_scales": w2p[1],
        "sa": (np.random.uniform(0.5, 1.6, (R, 1))).astype(np.float32),
        "vs_words": vsp[0],
        "vs_scales": vsp[1],
        "offs": striped(idx),
        "offs2": striped8(idx2),
        "offs3": striped8(idx3),
        "offs4": striped8(idx4),
        "offs5": striped8(idx5),
        "offs6": striped(idx6),
    }


def reference(xt_words, xt_scales, w_words, w_scales, w2_words, w2_scales, sa, vs_words, vs_scales, offs, offs2, offs3, offs4, offs5, offs6):
    idx = unstriped(offs)
    idx2 = unstriped8(offs2)
    idx3 = unstriped8(offs3)
    idx4 = unstriped8(offs4)
    idx5 = unstriped8(offs5)
    idx6 = unstriped(offs6)
    xtu = unpack_weight(xt_words, xt_scales, "e4m3")
    wu = unpack_weight(w_words, w_scales, "e2m1")
    w2u = unpack_weight(w2_words, w2_scales, "e4m3")
    vsu = unpack_weight(vs_words, vs_scales, "e4m3")
    xtidxg = xtu[:, idx]
    a = wu.T @ xtidxg
    b = w2u.T @ xtidxg
    pw = np.zeros((R, C))
    pw[np.arange(R)[:, None], idx2[np.arange(R) % 512 // 64]] = a
    pv = np.zeros((R, C))
    pv[np.arange(R)[:, None], idx3[np.arange(R) % 512 // 64]] = b
    pg = pw + pv
    pu = np.zeros((R, D))
    pu[np.arange(R)[:, None], idx4[np.arange(R) % 512 // 64]] = pg
    hid = pick8(pu, idx5, 64) * f64(sa)
    vsidx6g = vsu[:, idx6]
    hidq = mxq(hid, 0, "e4m3")
    y = vsidx6g.T @ hidq
    return y

@@ -1,0 +1,211 @@
+from contextlib import ExitStack
+
+import concourse.mybir as mybir
+
+K, J, R, T, C, D, O, N, S = 512, 256, 512, 512, 512, 1024, 256, 256, 1024
+FLOPS = 2 * K * R * J * 2 + 2 * R * N * O
+
+F32 = mybir.dt.float32
+BF16 = mybir.dt.bfloat16
+I32 = mybir.dt.int32
+U32 = mybir.dt.uint32
+U16 = mybir.dt.uint16
+U8 = mybir.dt.uint8
+FP8X4 = mybir.dt.float8_e4m3fn_x4
+FP4X4 = mybir.dt.float4_e2m1fn_x4
+COPY = mybir.ActivationFunctionType.Copy
+ADD = mybir.AluOpType.add
+
+P = 128
+PACK = 4
+QUADRANT = 32
+HALF = O // 2
+
+
+def tile_picked_tokens_plain_twin_widened_store_plain_kernel(
+    tc, xt_words, xt_scales, w_words, w_scales, w2_words, w2_scales, sa, vs_words, vs_scales,
+    offs, offs2, offs3, offs4, offs5, offs6, out,
+):
+    nc = tc.nc
+    with ExitStack() as ctx:
+        lists = ctx.enter_context(tc.tile_pool(name="lists", bufs=1))
+        sb = ctx.enter_context(tc.tile_pool(name="sb", bufs=1))
+        psum = ctx.enter_context(tc.psum_pool(name="psum", bufs=1))
+
+        def load_list(src, name):
+            tile = lists.tile(list(src.shape), U16, name=name)
+            nc.sync.dma_start(tile[:], src)
+            return tile
+
+        def load_words(queue, src, name):
+            flat = src[0].rearrange("p n t -> p (n t)").bitcast(I32)
+            tile = sb.tile([P, flat.shape[1]], I32, name=name, align_bytes=64)
+            queue.dma_start(tile[:], flat)
+            return tile
+
+        def load_scale_rows(queue, src, name):
+            rows = src[0].bitcast(I32).rearrange("(q r) c -> r q c", r=PACK)
+            tile = sb.tile(list(rows.shape), I32, name=name, align_bytes=64)
+            queue.dma_start(tile[:], rows)
+            return tile
+
+        def zeroed(shape, dtype, name, tag=None):
+            tile = sb.tile(shape, dtype, name=name, tag=tag or name, align_bytes=64)
+            if dtype == U8:
+                nc.vector.memset(tile[:].bitcast(I32), 0)
+            else:
+                nc.vector.memset(tile[:], 0.0)
+            return tile
+
+        def spread(plane, rows):
+            for q in range(PACK):
+                nc.vector.tensor_copy(plane[QUADRANT * q : QUADRANT * q + PACK, :].bitcast(I32), rows[:, q, :])
+
+        def load_plane(src, name):
+            tile = sb.tile([P, src.shape[2]], U8, name=name, align_bytes=64)
+            nc.gpsimd.memset(tile[:].bitcast(I32), 0)
+            for q in range(PACK):
+                nc.sync.dma_start(
+                    tile[QUADRANT * q : QUADRANT * q + PACK, :].bitcast(I32),
+                    src[0, PACK * q : PACK * (q + 1), :].bitcast(I32),
+                )
+            return tile
+
+        xt_raw = load_words(nc.scalar, xt_words, "xt_raw")
+        tok_list = load_list(offs, "tok_list")
+        xt_rows = load_scale_rows(nc.sync, xt_scales, "xt_rows")
+        w_rows = load_scale_rows(nc.sync, w_scales, "w_rows")
+        w_raw = sb.tile([P, 2 * R], U8, name="w_raw", align_bytes=64)
+        nc.scalar.dma_start(w_raw[:].bitcast(I32), w_words[0].bitcast(I32))
+        a_list = load_list(offs2, "a_list")
+        w2_raw = load_words(nc.sync, w2_words, "w2_raw")
+        w2_plane = load_plane(w2_scales, "w2_plane")
+        b_list = load_list(offs3, "b_list")
+        wide_list = load_list(offs4, "wide_list")
+        place_list = load_list(offs5, "place_list")
+        sa_sb = sb.tile([P, PACK], F32, name="sa_sb", align_bytes=64)
+        nc.sync.dma_start(sa_sb[:], sa.rearrange("(p t) o -> p (t o)", t=PACK))
+        entry_list = load_list(offs6, "entry_list")
+        vs_plane = load_plane(vs_scales, "vs_plane")
+        vs_raw = load_words(nc.sync, vs_words, "vs_raw")
+
+        xt_plane = zeroed([P, T], U8, "xt_plane")
+        w_plane = zeroed([P, R], U8, "w_plane")
+        pw = [zeroed([P, C], F32, "pw%d" % i) for i in range(2)]
+        pv = [zeroed([P, C], F32, "pv%d" % i) for i in range(2)]
+
+        spread(xt_plane, xt_rows)
+        spread(w_plane, w_rows)
+        xg_scales = sb.tile([P, J], U8, name="xg_scales", align_bytes=64)
+        nc.vector.tensor_copy(xg_scales[:], xt_plane[:].indirect(tok_list[:]))
+        w_dealt = [sb.tile([P, 2 * P], U8, name="w_dealt%d" % t, align_bytes=64) for t in range(PACK)]
+        w_dealt_scales = [sb.tile([P, P], U8, name="w_dealt_scales%d" % t, align_bytes=64) for t in range(PACK)]
+        w2_dealt = [sb.tile([P, P], U32, name="w2_dealt%d" % t, align_bytes=64) for t in range(PACK)]
+        w2_dealt_scales = [sb.tile([P, P], U8, name="w2_dealt_scales%d" % t, align_bytes=64) for t in range(PACK)]
+
+        def every_fourth(ap, t):
+            return ap.rearrange("p (m t) -> p t m", t=PACK)[:, t, :]
+
+        xg_words = sb.tile([P, J], U32, name="xg_words", align_bytes=64)
+        nc.vector.tensor_copy(xg_words[:], xt_raw[:].bitcast(U32).indirect(tok_list[:]))
+        for t in range(PACK):
+            nc.scalar.copy(w_dealt[t][:].bitcast(U16), every_fourth(w_raw[:].bitcast(U16), t))
+
+        def product(words, scales, bank, name):
+            acc = psum.tile([P, J], F32, name=name + "_acc", tag="bank%d" % bank)
+            nc.tensor.matmul_mx(
+                out=acc[:], lhsT=words, lhsT_scale=scales, rhs=xg_words[:].bitcast(FP8X4), rhs_scale=xg_scales[:],
+                start=True, stop=True,
+            )
+            res = sb.tile([P, J], F32, name=name, tag=name, align_bytes=64)
+            nc.vector.tensor_copy(res[:], acc[:])
+            return res
+
+        def first(t):
+            nc.gpsimd.tensor_copy(w_dealt_scales[t][:], every_fourth(w_plane[:], t))
+            return product(w_dealt[t][:].bitcast(FP4X4), w_dealt_scales[t][:], t, "a%d" % t)
+
+        def second(t):
+            nc.gpsimd.tensor_copy(w2_dealt[t][:], every_fourth(w2_raw[:].bitcast(U32), t))
+            nc.gpsimd.tensor_copy(w2_dealt_scales[t][:], every_fourth(w2_plane[:], t))
+            return product(w2_dealt[t][:].bitcast(FP8X4), w2_dealt_scales[t][:], PACK + t, "b%d" % t)
+
+        a = [first(0), first(1)]
+        b = [second(0), second(1)]
+        a.extend([first(2), first(3)])
+        b.extend([second(2), second(3)])
+
+        hid = sb.tile([P, PACK, O], BF16, name="hid", align_bytes=64)
+        pu = {}
+        pg = {}
+
+        def put_a(t):
+            nc.scalar.activation(pw[t % 2][:].indirect(a_list[:]), a[t][:], COPY)
+
+        def put_b(t):
+            nc.scalar.activation(pv[t % 2][:].indirect(b_list[:]), b[t][:], COPY)
+
+        def add_boards(t, tag):
+            pg[t] = sb.tile([P, C], F32, name="pg%d" % t, tag=tag, align_bytes=64)
+            nc.vector.tensor_tensor(pg[t][:], pw[t % 2][:], pv[t % 2][:], ADD)
+
+        def put_wide(t):
+            nc.scalar.activation(pu[t % 2][:].indirect(wide_list[:]), pg[t][:], COPY)
+
+        def fetch(t):
+            nc.scalar.activation(hid[:, t, :], pu[t % 2][:].indirect(place_list[:]), COPY, scale=sa_sb[:, t : t + 1])
+
+        put_a(0)
+        put_a(1)
+        pu[0] = zeroed([P, D], F32, "pu0", tag="a0")
+        put_b(0)
+        pu[1] = zeroed([P, D], F32, "pu1", tag="a1")
+        put_b(1)
+        add_boards(0, "pg0")
+        put_wide(0)
+        add_boards(1, "pg1")
+        put_a(2)
+        fetch(0)
+        put_b(2)
+        put_wide(1)
+        put_a(3)
+        fetch(1)
+        put_b(3)
+        add_boards(2, "a3")
+        put_wide(2)
+        add_boards(3, "pg3")
+        put_wide(3)
+        fetch(2)
+        fetch(3)
+
+        vg_scales = sb.tile([P, N], U8, name="vg_scales", align_bytes=64)
+        vg_words = sb.tile([P, N], U32, name="vg_words", align_bytes=64)
+        nc.vector.tensor_copy(vg_scales[:], vs_plane[:].indirect(entry_list[:]))
+        nc.vector.tensor_copy(vg_words[:], vs_raw[:].bitcast(U32).indirect(entry_list[:]))
+
+        woven, codes, scales = [], [], []
+        for h in range(2):
+            woven.append(sb.tile([P, HALF * PACK], BF16, name="woven%d" % h, align_bytes=64))
+            nc.vector.tensor_copy(
+                woven[h][:].rearrange("p (c i t) -> p c t i", i=4, t=PACK),
+                hid[:, :, h * HALF : (h + 1) * HALF].rearrange("p t (c i) -> p c t i", i=4),
+            )
+        for h in range(2):
+            codes.append(sb.tile([P, HALF], U32, name="codes%d" % h, align_bytes=64))
+            scales.append(sb.tile([P, HALF], U8, name="scales%d" % h, align_bytes=64))
+            nc.vector.quantize_mx(out=codes[h][:].bitcast(FP8X4), scales=scales[h][:], in_=woven[h][:])
+        for h in range(2):
+            for m in range(N // P):
+                rows = slice(m * P, (m + 1) * P)
+                acc = psum.tile([P, HALF], F32, name="y_acc%d%d" % (h, m), tag="bank%d" % (2 * h + m))
+                nc.tensor.matmul_mx(
+                    out=acc[:], lhsT=vg_words[:, rows].bitcast(FP8X4), lhsT_scale=vg_scales[:, rows],
+                    rhs=codes[h][:].bitcast(FP8X4), rhs_scale=scales[h][:], start=True, stop=True,
+                )
+                y = sb.tile([P, HALF], F32, name="y%d%d" % (h, m), align_bytes=64)
+                if h == 1 and m == 0:
+                    nc.vector.tensor_copy(y[:], acc[:])
+                else:
+                    nc.scalar.copy(y[:], acc[:])
+                queue = nc.scalar if (h == 1 and m == 1) else nc.sync
+                queue.dma_start(out[rows, h * HALF : (h + 1) * HALF], y[:])

@@ -49,55 +49,52 @@ def tile_picked_tokens_plain_twin_widened_store_plain_kernel(
             queue.dma_start(tile[:], rows)
             return tile
 
-        def zeroed(shape, dtype, name, tag=None):
+        def zeroed(shape, dtype, name, tag=None, engine=nc.vector):
             tile = sb.tile(shape, dtype, name=name, tag=tag or name, align_bytes=64)
             if dtype == U8:
                 nc.vector.memset(tile[:].bitcast(I32), 0)
             else:
-                nc.vector.memset(tile[:], 0.0)
+                engine.memset(tile[:], 0.0)
             return tile
 
         def spread(plane, rows):
             for q in range(PACK):
                 nc.vector.tensor_copy(plane[QUADRANT * q : QUADRANT * q + PACK, :].bitcast(I32), rows[:, q, :])
 
-        def load_plane(src, name):
+        def load_plane(src, name, queues):
             tile = sb.tile([P, src.shape[2]], U8, name=name, align_bytes=64)
             nc.gpsimd.memset(tile[:].bitcast(I32), 0)
             for q in range(PACK):
-                nc.sync.dma_start(
+                queues[q].dma_start(
                     tile[QUADRANT * q : QUADRANT * q + PACK, :].bitcast(I32),
                     src[0, PACK * q : PACK * (q + 1), :].bitcast(I32),
                 )
             return tile
 
-        xt_raw = load_words(nc.scalar, xt_words, "xt_raw")
-        tok_list = load_list(offs, "tok_list")
-        xt_rows = load_scale_rows(nc.sync, xt_scales, "xt_rows")
         w_rows = load_scale_rows(nc.sync, w_scales, "w_rows")
+        xt_raw = load_words(nc.scalar, xt_words, "xt_raw")
+        xt_plane = load_plane(xt_scales, "xt_plane", [nc.sync, nc.scalar, nc.sync, nc.scalar])
+        tok_list = load_list(offs, "tok_list")
         w_raw = sb.tile([P, 2 * R], U8, name="w_raw", align_bytes=64)
         nc.scalar.dma_start(w_raw[:].bitcast(I32), w_words[0].bitcast(I32))
         a_list = load_list(offs2, "a_list")
         w2_raw = load_words(nc.sync, w2_words, "w2_raw")
-        w2_plane = load_plane(w2_scales, "w2_plane")
+        w2_plane = load_plane(w2_scales, "w2_plane", [nc.sync] * PACK)
         b_list = load_list(offs3, "b_list")
         wide_list = load_list(offs4, "wide_list")
+        entry_list = load_list(offs6, "entry_list")
+        vs_plane = load_plane(vs_scales, "vs_plane", [nc.sync] * PACK)
+        vs_raw = load_words(nc.sync, vs_words, "vs_raw")
         place_list = load_list(offs5, "place_list")
         sa_sb = sb.tile([P, PACK], F32, name="sa_sb", align_bytes=64)
         nc.sync.dma_start(sa_sb[:], sa.rearrange("(p t) o -> p (t o)", t=PACK))
-        entry_list = load_list(offs6, "entry_list")
-        vs_plane = load_plane(vs_scales, "vs_plane")
-        vs_raw = load_words(nc.sync, vs_words, "vs_raw")
 
-        xt_plane = zeroed([P, T], U8, "xt_plane")
         w_plane = zeroed([P, R], U8, "w_plane")
         pw = [zeroed([P, C], F32, "pw%d" % i) for i in range(2)]
-        pv = [zeroed([P, C], F32, "pv%d" % i) for i in range(2)]
+        pv = [zeroed([P, C], F32, "pv%d" % i, engine=nc.gpsimd) for i in range(2)]
 
-        spread(xt_plane, xt_rows)
         spread(w_plane, w_rows)
         xg_scales = sb.tile([P, J], U8, name="xg_scales", align_bytes=64)
-        nc.vector.tensor_copy(xg_scales[:], xt_plane[:].indirect(tok_list[:]))
         w_dealt = [sb.tile([P, 2 * P], U8, name="w_dealt%d" % t, align_bytes=64) for t in range(PACK)]
         w_dealt_scales = [sb.tile([P, P], U8, name="w_dealt_scales%d" % t, align_bytes=64) for t in range(PACK)]
         w2_dealt = [sb.tile([P, P], U32, name="w2_dealt%d" % t, align_bytes=64) for t in range(PACK)]
@@ -107,33 +104,49 @@ def tile_picked_tokens_plain_twin_widened_store_plain_kernel(
             return ap.rearrange("p (m t) -> p t m", t=PACK)[:, t, :]
 
         xg_words = sb.tile([P, J], U32, name="xg_words", align_bytes=64)
-        nc.vector.tensor_copy(xg_words[:], xt_raw[:].bitcast(U32).indirect(tok_list[:]))
+        nc.vector.tensor_copy(w_dealt_scales[0][:], every_fourth(w_plane[:], 0))
+        for h in range(2):
+            slots = slice(h * J // 2, (h + 1) * J // 2)
+            part = tok_list[:, h * J // 32 : (h + 1) * J // 32]
+            nc.vector.tensor_copy(xg_scales[:, slots], xt_plane[:].indirect(part))
+            nc.vector.tensor_copy(xg_words[:, slots], xt_raw[:].bitcast(U32).indirect(part))
         for t in range(PACK):
             nc.scalar.copy(w_dealt[t][:].bitcast(U16), every_fourth(w_raw[:].bitcast(U16), t))
 
-        def product(words, scales, bank, name):
-            acc = psum.tile([P, J], F32, name=name + "_acc", tag="bank%d" % bank)
+        banks = []
+
+        def product(words, scales, slots, name):
+            width = slots.stop - slots.start
+            acc = psum.tile([P, width], F32, name=name + "_acc", tag="bank%d" % (len(banks) % 8))
+            banks.append(acc)
             nc.tensor.matmul_mx(
-                out=acc[:], lhsT=words, lhsT_scale=scales, rhs=xg_words[:].bitcast(FP8X4), rhs_scale=xg_scales[:],
+                out=acc[:], lhsT=words, lhsT_scale=scales,
+                rhs=xg_words[:, slots].bitcast(FP8X4), rhs_scale=xg_scales[:, slots],
                 start=True, stop=True,
             )
-            res = sb.tile([P, J], F32, name=name, tag=name, align_bytes=64)
+            res = sb.tile([P, width], F32, name=name, tag=name, align_bytes=64)
             nc.vector.tensor_copy(res[:], acc[:])
             return res
 
-        def first(t):
-            nc.gpsimd.tensor_copy(w_dealt_scales[t][:], every_fourth(w_plane[:], t))
-            return product(w_dealt[t][:].bitcast(FP4X4), w_dealt_scales[t][:], t, "a%d" % t)
+        def first(t, slots, name):
+            return product(w_dealt[t][:].bitcast(FP4X4), w_dealt_scales[t][:], slots, name)
 
         def second(t):
             nc.gpsimd.tensor_copy(w2_dealt[t][:], every_fourth(w2_raw[:].bitcast(U32), t))
             nc.gpsimd.tensor_copy(w2_dealt_scales[t][:], every_fourth(w2_plane[:], t))
-            return product(w2_dealt[t][:].bitcast(FP8X4), w2_dealt_scales[t][:], PACK + t, "b%d" % t)
+            return product(w2_dealt[t][:].bitcast(FP8X4), w2_dealt_scales[t][:], slice(0, J), "b%d" % t)
 
-        a = [first(0), first(1)]
-        b = [second(0), second(1)]
-        a.extend([first(2), first(3)])
-        b.extend([second(2), second(3)])
+        for t in range(1, PACK):
+            nc.gpsimd.tensor_copy(w_dealt_scales[t][:], every_fourth(w_plane[:], t))
+        a, b = {}, {}
+        a0_first = first(0, slice(0, J // 2), "a0_first")
+        a[1] = first(1, slice(0, J), "a1")
+        a0_second = first(0, slice(J // 2, J), "a0_second")
+        b[0] = second(0)
+        b[1] = second(1)
+        for t in range(2, PACK):
+            a[t] = first(t, slice(0, J), "a%d" % t)
+            b[t] = second(t)
 
         hid = sb.tile([P, PACK, O], BF16, name="hid", align_bytes=64)
         pu = {}
@@ -155,28 +168,23 @@ def tile_picked_tokens_plain_twin_widened_store_plain_kernel(
         def fetch(t):
             nc.scalar.activation(hid[:, t, :], pu[t % 2][:].indirect(place_list[:]), COPY, scale=sa_sb[:, t : t + 1])
 
-        put_a(0)
+        nc.scalar.activation(pw[0][:].indirect(a_list[:, 0 : J // 32]), a0_first[:], COPY)
+        pu[0] = zeroed([P, D], F32, "pu0", tag="w_dealt1")
+        pu[1] = zeroed([P, D], F32, "pu1", tag="w_dealt3")
         put_a(1)
-        pu[0] = zeroed([P, D], F32, "pu0", tag="a0")
+        nc.scalar.activation(pw[0][:].indirect(a_list[:, J // 32 : J // 16]), a0_second[:], COPY)
         put_b(0)
-        pu[1] = zeroed([P, D], F32, "pu1", tag="a1")
         put_b(1)
-        add_boards(0, "pg0")
+        for t in range(PACK):
+            add_boards(t, "pg%d" % t)
+            if t + 2 < PACK:
+                put_a(t + 2)
+                put_b(t + 2)
         put_wide(0)
-        add_boards(1, "pg1")
-        put_a(2)
-        fetch(0)
-        put_b(2)
-        put_wide(1)
-        put_a(3)
-        fetch(1)
-        put_b(3)
-        add_boards(2, "a3")
-        put_wide(2)
-        add_boards(3, "pg3")
-        put_wide(3)
-        fetch(2)
-        fetch(3)
+        for t in range(PACK):
+            if t + 1 < PACK:
+                put_wide(t + 1)
+            fetch(t)
 
         vg_scales = sb.tile([P, N], U8, name="vg_scales", align_bytes=64)
         vg_words = sb.tile([P, N], U32, name="vg_words", align_bytes=64)
@@ -197,7 +205,7 @@ def tile_picked_tokens_plain_twin_widened_store_plain_kernel(
         for h in range(2):
             for m in range(N // P):
                 rows = slice(m * P, (m + 1) * P)
-                acc = psum.tile([P, HALF], F32, name="y_acc%d%d" % (h, m), tag="bank%d" % (2 * h + m))
+                acc = psum.tile([P, HALF], F32, name="y_acc%d%d" % (h, m), tag="bank%d" % (2 + 2 * h + m))
                 nc.tensor.matmul_mx(
                     out=acc[:], lhsT=vg_words[:, rows].bitcast(FP8X4), lhsT_scale=vg_scales[:, rows],
                     rhs=codes[h][:].bitcast(FP8X4), rhs_scale=scales[h][:], start=True, stop=True,

from contextlib import ExitStack

import concourse.mybir as mybir

K, J, R, T, C, D, O, N, S = 512, 256, 512, 512, 512, 1024, 256, 256, 1024
FLOPS = 2 * K * R * J * 2 + 2 * R * N * O

F32 = mybir.dt.float32
BF16 = mybir.dt.bfloat16
I32 = mybir.dt.int32
U32 = mybir.dt.uint32
U16 = mybir.dt.uint16
U8 = mybir.dt.uint8
FP8X4 = mybir.dt.float8_e4m3fn_x4
FP4X4 = mybir.dt.float4_e2m1fn_x4
COPY = mybir.ActivationFunctionType.Copy
ADD = mybir.AluOpType.add

P = 128
PACK = 4
QUADRANT = 32
HALF = O // 2


def tile_picked_tokens_plain_twin_widened_store_plain_kernel(
    tc, xt_words, xt_scales, w_words, w_scales, w2_words, w2_scales, sa, vs_words, vs_scales,
    offs, offs2, offs3, offs4, offs5, offs6, out,
):
    nc = tc.nc
    with ExitStack() as ctx:
        lists = ctx.enter_context(tc.tile_pool(name="lists", bufs=1))
        sb = ctx.enter_context(tc.tile_pool(name="sb", bufs=1))
        psum = ctx.enter_context(tc.psum_pool(name="psum", bufs=1))

        def load_list(src, name):
            tile = lists.tile(list(src.shape), U16, name=name)
            nc.sync.dma_start(tile[:], src)
            return tile

        def load_words(queue, src, name):
            flat = src[0].rearrange("p n t -> p (n t)").bitcast(I32)
            tile = sb.tile([P, flat.shape[1]], I32, name=name, align_bytes=64)
            queue.dma_start(tile[:], flat)
            return tile

        def load_scale_rows(queue, src, name):
            rows = src[0].bitcast(I32).rearrange("(q r) c -> r q c", r=PACK)
            tile = sb.tile(list(rows.shape), I32, name=name, align_bytes=64)
            queue.dma_start(tile[:], rows)
            return tile

        def zeroed(shape, dtype, name, tag=None, engine=nc.vector):
            tile = sb.tile(shape, dtype, name=name, tag=tag or name, align_bytes=64)
            if dtype == U8:
                nc.vector.memset(tile[:].bitcast(I32), 0)
            else:
                engine.memset(tile[:], 0.0)
            return tile

        def spread(plane, rows):
            for q in range(PACK):
                nc.vector.tensor_copy(plane[QUADRANT * q : QUADRANT * q + PACK, :].bitcast(I32), rows[:, q, :])

        def load_plane(src, name, queues):
            tile = sb.tile([P, src.shape[2]], U8, name=name, align_bytes=64)
            nc.gpsimd.memset(tile[:].bitcast(I32), 0)
            for q in range(PACK):
                queues[q].dma_start(
                    tile[QUADRANT * q : QUADRANT * q + PACK, :].bitcast(I32),
                    src[0, PACK * q : PACK * (q + 1), :].bitcast(I32),
                )
            return tile

        w_rows = load_scale_rows(nc.sync, w_scales, "w_rows")
        xt_raw = load_words(nc.scalar, xt_words, "xt_raw")
        xt_plane = load_plane(xt_scales, "xt_plane", [nc.sync, nc.scalar, nc.sync, nc.scalar])
        tok_list = load_list(offs, "tok_list")
        w_raw = sb.tile([P, 2 * R], U8, name="w_raw", align_bytes=64)
        nc.scalar.dma_start(w_raw[:].bitcast(I32), w_words[0].bitcast(I32))
        a_list = load_list(offs2, "a_list")
        w2_raw = load_words(nc.sync, w2_words, "w2_raw")
        w2_plane = load_plane(w2_scales, "w2_plane", [nc.sync] * PACK)
        b_list = load_list(offs3, "b_list")
        wide_list = load_list(offs4, "wide_list")
        entry_list = load_list(offs6, "entry_list")
        vs_plane = load_plane(vs_scales, "vs_plane", [nc.sync] * PACK)
        vs_raw = load_words(nc.sync, vs_words, "vs_raw")
        place_list = load_list(offs5, "place_list")
        sa_sb = sb.tile([P, PACK], F32, name="sa_sb", align_bytes=64)
        nc.sync.dma_start(sa_sb[:], sa.rearrange("(p t) o -> p (t o)", t=PACK))

        w_plane = zeroed([P, R], U8, "w_plane")
        pw = [zeroed([P, C], F32, "pw%d" % i) for i in range(2)]
        pv = [zeroed([P, C], F32, "pv%d" % i, engine=nc.gpsimd) for i in range(2)]

        spread(w_plane, w_rows)
        xg_scales = sb.tile([P, J], U8, name="xg_scales", align_bytes=64)
        w_dealt = [sb.tile([P, 2 * P], U8, name="w_dealt%d" % t, align_bytes=64) for t in range(PACK)]
        w_dealt_scales = [sb.tile([P, P], U8, name="w_dealt_scales%d" % t, align_bytes=64) for t in range(PACK)]
        w2_dealt = [sb.tile([P, P], U32, name="w2_dealt%d" % t, align_bytes=64) for t in range(PACK)]
        w2_dealt_scales = [sb.tile([P, P], U8, name="w2_dealt_scales%d" % t, align_bytes=64) for t in range(PACK)]

        def every_fourth(ap, t):
            return ap.rearrange("p (m t) -> p t m", t=PACK)[:, t, :]

        xg_words = sb.tile([P, J], U32, name="xg_words", align_bytes=64)
        nc.vector.tensor_copy(w_dealt_scales[0][:], every_fourth(w_plane[:], 0))
        for h in range(2):
            slots = slice(h * J // 2, (h + 1) * J // 2)
            part = tok_list[:, h * J // 32 : (h + 1) * J // 32]
            nc.vector.tensor_copy(xg_scales[:, slots], xt_plane[:].indirect(part))
            nc.vector.tensor_copy(xg_words[:, slots], xt_raw[:].bitcast(U32).indirect(part))
        for t in range(PACK):
            nc.scalar.copy(w_dealt[t][:].bitcast(U16), every_fourth(w_raw[:].bitcast(U16), t))

        banks = []

        def product(words, scales, slots, name):
            width = slots.stop - slots.start
            acc = psum.tile([P, width], F32, name=name + "_acc", tag="bank%d" % (len(banks) % 8))
            banks.append(acc)
            nc.tensor.matmul_mx(
                out=acc[:], lhsT=words, lhsT_scale=scales,
                rhs=xg_words[:, slots].bitcast(FP8X4), rhs_scale=xg_scales[:, slots],
                start=True, stop=True,
            )
            res = sb.tile([P, width], F32, name=name, tag=name, align_bytes=64)
            nc.vector.tensor_copy(res[:], acc[:])
            return res

        def first(t, slots, name):
            return product(w_dealt[t][:].bitcast(FP4X4), w_dealt_scales[t][:], slots, name)

        def second(t):
            nc.gpsimd.tensor_copy(w2_dealt[t][:], every_fourth(w2_raw[:].bitcast(U32), t))
            nc.gpsimd.tensor_copy(w2_dealt_scales[t][:], every_fourth(w2_plane[:], t))
            return product(w2_dealt[t][:].bitcast(FP8X4), w2_dealt_scales[t][:], slice(0, J), "b%d" % t)

        for t in range(1, PACK):
            nc.gpsimd.tensor_copy(w_dealt_scales[t][:], every_fourth(w_plane[:], t))
        a, b = {}, {}
        a0_first = first(0, slice(0, J // 2), "a0_first")
        a[1] = first(1, slice(0, J), "a1")
        a0_second = first(0, slice(J // 2, J), "a0_second")
        b[0] = second(0)
        b[1] = second(1)
        for t in range(2, PACK):
            a[t] = first(t, slice(0, J), "a%d" % t)
            b[t] = second(t)

        hid = sb.tile([P, PACK, O], BF16, name="hid", align_bytes=64)
        pu = {}
        pg = {}

        def put_a(t):
            nc.scalar.activation(pw[t % 2][:].indirect(a_list[:]), a[t][:], COPY)

        def put_b(t):
            nc.scalar.activation(pv[t % 2][:].indirect(b_list[:]), b[t][:], COPY)

        def add_boards(t, tag):
            pg[t] = sb.tile([P, C], F32, name="pg%d" % t, tag=tag, align_bytes=64)
            nc.vector.tensor_tensor(pg[t][:], pw[t % 2][:], pv[t % 2][:], ADD)

        def put_wide(t):
            nc.scalar.activation(pu[t % 2][:].indirect(wide_list[:]), pg[t][:], COPY)

        def fetch(t):
            nc.scalar.activation(hid[:, t, :], pu[t % 2][:].indirect(place_list[:]), COPY, scale=sa_sb[:, t : t + 1])

        nc.scalar.activation(pw[0][:].indirect(a_list[:, 0 : J // 32]), a0_first[:], COPY)
        pu[0] = zeroed([P, D], F32, "pu0", tag="w_dealt1")
        pu[1] = zeroed([P, D], F32, "pu1", tag="w_dealt3")
        put_a(1)
        nc.scalar.activation(pw[0][:].indirect(a_list[:, J // 32 : J // 16]), a0_second[:], COPY)
        put_b(0)
        put_b(1)
        for t in range(PACK):
            add_boards(t, "pg%d" % t)
            if t + 2 < PACK:
                put_a(t + 2)
                put_b(t + 2)
        put_wide(0)
        for t in range(PACK):
            if t + 1 < PACK:
                put_wide(t + 1)
            fetch(t)

        vg_scales = sb.tile([P, N], U8, name="vg_scales", align_bytes=64)
        vg_words = sb.tile([P, N], U32, name="vg_words", align_bytes=64)
        nc.vector.tensor_copy(vg_scales[:], vs_plane[:].indirect(entry_list[:]))
        nc.vector.tensor_copy(vg_words[:], vs_raw[:].bitcast(U32).indirect(entry_list[:]))

        woven, codes, scales = [], [], []
        for h in range(2):
            woven.append(sb.tile([P, HALF * PACK], BF16, name="woven%d" % h, align_bytes=64))
            nc.vector.tensor_copy(
                woven[h][:].rearrange("p (c i t) -> p c t i", i=4, t=PACK),
                hid[:, :, h * HALF : (h + 1) * HALF].rearrange("p t (c i) -> p c t i", i=4),
            )
        for h in range(2):
            codes.append(sb.tile([P, HALF], U32, name="codes%d" % h, align_bytes=64))
            scales.append(sb.tile([P, HALF], U8, name="scales%d" % h, align_bytes=64))
            nc.vector.quantize_mx(out=codes[h][:].bitcast(FP8X4), scales=scales[h][:], in_=woven[h][:])
        for h in range(2):
            for m in range(N // P):
                rows = slice(m * P, (m + 1) * P)
                acc = psum.tile([P, HALF], F32, name="y_acc%d%d" % (h, m), tag="bank%d" % (2 + 2 * h + m))
                nc.tensor.matmul_mx(
                    out=acc[:], lhsT=vg_words[:, rows].bitcast(FP8X4), lhsT_scale=vg_scales[:, rows],
                    rhs=codes[h][:].bitcast(FP8X4), rhs_scale=scales[h][:], start=True, stop=True,
                )
                y = sb.tile([P, HALF], F32, name="y%d%d" % (h, m), align_bytes=64)
                if h == 1 and m == 0:
                    nc.vector.tensor_copy(y[:], acc[:])
                else:
                    nc.scalar.copy(y[:], acc[:])
                queue = nc.scalar if (h == 1 and m == 1) else nc.sync
                queue.dma_start(out[rows, h * HALF : (h + 1) * HALF], y[:])
